import numpy as np
import ml_dtypes


def mxq(x, axis, fmt="e4m3"):
    dtype, down = {"e4m3": (ml_dtypes.float8_e4m3fn, 7), "e5m2": (ml_dtypes.float8_e5m2, 14)}[fmt]
    v = np.moveaxis(np.asarray(x, np.float32).astype(ml_dtypes.bfloat16).astype(np.float64), axis, -1)
    blocks = v.reshape(v.shape[:-1] + (-1, 32))
    amax = np.abs(blocks).max(-1, keepdims=True)
    byte = np.maximum(np.where(amax > 0, np.frexp(amax)[1] - 1 + 127, 0) - down, 1)
    scale = np.exp2(byte - 127.0)
    codes = (blocks / scale).astype(np.float32).astype(dtype).astype(np.float64)
    return np.moveaxis((codes * scale).reshape(v.shape), -1, axis)


WIDE = False


def mx_kscale(k):
    if not WIDE:
        return np.ones(k)
    levels = np.array([10, -10, 5, -5, 0])
    if k % 512:
        return np.exp2(np.random.permutation(np.resize(levels, k // 32))).repeat(32)
    a = np.empty((k // 512, 16))
    for p in range(k // 512):
        a[p, :8] = np.random.permutation(np.resize(levels, 8))
        for g in range(8):
            far = levels[np.abs(levels - a[p, g]) >= 10]
            a[p, g + 8] = far[np.random.randint(len(far))]
    return np.exp2(a.ravel()).repeat(32)


def f64(x):
    return np.asarray(x).astype(np.float64)


def striped(idx):
    return np.tile(idx.reshape(-1, 16).T, (8, 1)).astype(np.uint16)


def unstriped(offs):
    return offs[:16].T.reshape(-1).astype(np.int64)


def pack_weight(w):
    k, n = w.shape
    w = f64(np.asarray(w, np.float32).astype(ml_dtypes.bfloat16)).reshape(k // 32, 32, n)
    amax = np.abs(w).max(1)
    byte = np.clip(np.where(amax > 0, np.frexp(amax)[1] - 1 + 127 - 7, 1), 1, 254)
    scaled = (w * np.exp2(127.0 - byte)[:, None, :]).reshape(k, n).astype(np.float32)
    words = np.ascontiguousarray(scaled.reshape(k // 512, 128, 4, n).transpose(0, 1, 3, 2)).astype(ml_dtypes.float8_e4m3fn).view(np.uint8)
    return words, np.ascontiguousarray(byte.astype(np.uint8).reshape(k // 512, 16, n))


def unpack_weight(words, scales):
    g, p, n, _ = words.shape
    vals = np.ascontiguousarray(words).view(ml_dtypes.float8_e4m3fn).astype(np.float64) * np.repeat(np.exp2(scales.astype(np.float64) - 127.0), 8, axis=1)[..., None]
    return vals.transpose(0, 1, 3, 2).reshape(g * 512, n)


def relu(v):
    return np.maximum(v, 0.0)


K, T, N = 1024, 1024, 128


def setup_inputs():
    n = np.random.standard_normal
    s = mx_kscale(K)[:, None]
    packed_xT = pack_weight(n((K, T)) * s)
    return {
        "x_words": packed_xT[0],
        "x_scales": packed_xT[1],
        "w1": (n((K, N)) / np.sqrt(K) / s).astype(np.float32),
        "pos1": striped(np.random.permutation(T)),
        "pos2": striped(np.random.permutation(T)),
        "pos3": striped(np.random.permutation(T)),
    }


def reference(x_words, x_scales, w1, pos1, pos2, pos3):
    xq = unpack_weight(x_words, x_scales)
    y = relu(mxq(f64(w1), 0, "e4m3").T @ xq)
    n0 = y[:, unstriped(pos1)]
    n1 = y[:, unstriped(pos2)]
    n2 = y[:, unstriped(pos3)]
    return np.maximum(np.minimum(n0, n1), np.minimum(np.maximum(n0, n1), n2))

@@ -1,0 +1,110 @@
+from contextlib import ExitStack
+
+import concourse.mybir as mybir
+
+K, T, M = 1024, 1024, 128
+FLOPS = 2 * K * T * M
+
+F32 = mybir.dt.float32
+BF16 = mybir.dt.bfloat16
+I32 = mybir.dt.int32
+U32 = mybir.dt.uint32
+U16 = mybir.dt.uint16
+U8 = mybir.dt.uint8
+FP8X4 = mybir.dt.float8_e4m3fn_x4
+ALU = mybir.AluOpType
+ACT = mybir.ActivationFunctionType
+
+P = 128
+PACK = 4
+PASSES = 2
+HALF = 512
+CHUNKS = (384, 384, 128, 128)
+
+
+def tile_picked_wmedian_relu_l_kernel(tc, x_words, x_scales, w1, pos1, pos2, pos3, out):
+    nc = tc.nc
+    with ExitStack() as ctx:
+        keep = ctx.enter_context(tc.tile_pool(name="keep", bufs=1))
+        psum = ctx.enter_context(tc.psum_pool(name="psum", bufs=1))
+
+        planes = keep.tile([P, T], U8, name="planes", align_bytes=64)
+        nc.vector.memset(planes[:].bitcast(I32), 0)
+        warm = keep.tile([P, 8], F32, name="warm")
+        warm_out = keep.tile([P, 8], F32, name="warm_out")
+        nc.gpsimd.memset(warm[:], 0.0)
+
+        w_raw = [keep.tile([P, PACK, M], F32, name="w_raw%d" % z) for z in range(PASSES)]
+        x_sb = [[keep.tile([P, HALF], I32, name="x%d%d" % (z, h), align_bytes=64) for h in range(2)] for z in range(PASSES)]
+        w_rows = w1.rearrange("(z p j) m -> z p j m", z=PASSES, j=PACK)
+        x_i32 = x_words.rearrange("z p c r -> z p (c r)").bitcast(I32)
+        s_i32 = x_scales.bitcast(I32)
+
+        for q in range(4):
+            nc.scalar.dma_start(out=planes[32 * q : 32 * q + 8, :].bitcast(I32), in_=s_i32[:, 4 * q : 4 * q + 4, :])
+        nc.scalar.activation(warm_out[:], warm[:], ACT.Relu)
+
+        nc.sync.dma_start(out=w_raw[0][:], in_=w_rows[0])
+        nc.sync.dma_start(out=x_sb[0][0][:], in_=x_i32[0][:, 0:HALF])
+        nc.sync.dma_start(out=w_raw[1][:], in_=w_rows[1])
+        nc.sync.dma_start(out=x_sb[1][0][:], in_=x_i32[1][:, 0:HALF])
+        nc.sync.dma_start(out=x_sb[0][1][:], in_=x_i32[0][:, HALF:T])
+        nc.sync.dma_start(out=x_sb[1][1][:], in_=x_i32[1][:, HALF:T])
+        lists = []
+        for i, pos in enumerate((pos1, pos2, pos3)):
+            offs = keep.tile([P, T // 16], U16, name="offs%d" % i)
+            nc.sync.dma_start(offs[:], pos)
+            lists.append(offs)
+
+        w_codes = []
+        w_scales = []
+        for z in range(PASSES):
+            grouped = keep.tile([P, M, PACK], BF16, name="grouped%d" % z, align_bytes=64)
+            nc.vector.tensor_copy(
+                out=grouped[:].rearrange("p (c i) j -> p c j i", i=4),
+                in_=w_raw[z][:].rearrange("p j (c i) -> p c j i", i=4),
+            )
+            codes = keep.tile([P, M], U32, name="w_codes%d" % z, align_bytes=64)
+            scales = keep.tile([P, M], U8, name="w_scales%d" % z, align_bytes=64)
+            nc.vector.quantize_mx(out=codes[:].bitcast(FP8X4), scales=scales[:], in_=grouped[:].rearrange("p m j -> p (m j)"))
+            w_codes.append(codes)
+            w_scales.append(scales)
+
+        y = keep.tile([P, T], F32, name="y")
+        Q = 256
+        groups = [(0, 0, HALF), (1, 0, Q), (1, Q, Q)]
+        for g, (h, c0, n) in enumerate(groups):
+            acc = psum.tile([P, n], F32, name="acc%d" % g)
+            for z in range(PASSES):
+                nc.tensor.matmul_mx(
+                    out=acc[:],
+                    lhsT=w_codes[z][:].bitcast(FP8X4),
+                    lhsT_scale=w_scales[z][:],
+                    rhs=x_sb[z][h][:, c0 : c0 + n].bitcast(FP8X4),
+                    rhs_scale=planes[4 * z : P, h * HALF + c0 : h * HALF + c0 + n],
+                    start=(z == 0),
+                    stop=(z == PASSES - 1),
+                )
+            dst = y[:, h * HALF + c0 : h * HALF + c0 + n]
+            if g == 2:
+                nc.vector.tensor_scalar(dst, acc[:], 0.0, None, ALU.max)
+            else:
+                nc.scalar.activation(dst, acc[:], ACT.Relu)
+
+        v0 = 0
+        for i, n in enumerate(CHUNKS):
+            got = []
+            for l in range(3):
+                gt = keep.tile([P, n], F32, name="g%d_%d" % (i, l))
+                nc.vector.tensor_copy(gt[:], y[:].indirect(lists[l][:, v0 // 16 : (v0 + n) // 16]))
+                got.append(gt)
+            lo = keep.tile([P, n], F32, name="lo%d" % i)
+            hi = keep.tile([P, n], F32, name="hi%d" % i)
+            up = keep.tile([P, n], F32, name="up%d" % i)
+            res = keep.tile([P, n], F32, name="res%d" % i)
+            nc.vector.tensor_tensor(hi[:], got[0][:], got[1][:], ALU.max)
+            nc.vector.tensor_tensor(lo[:], got[0][:], got[1][:], ALU.min)
+            nc.vector.tensor_tensor(up[:], hi[:], got[2][:], ALU.min)
+            nc.vector.tensor_tensor(res[:], lo[:], up[:], ALU.max)
+            nc.sync.dma_start(out=out[:, v0 : v0 + n], in_=res[:])
+            v0 = v0 + n

@@ -1,6 +1,7 @@
 from contextlib import ExitStack
 
 import concourse.mybir as mybir
+from concourse.masks import make_identity
 
 K, T, M = 1024, 1024, 128
 FLOPS = 2 * K * T * M
@@ -18,8 +19,9 @@ ACT = mybir.ActivationFunctionType
 P = 128
 PACK = 4
 PASSES = 2
-HALF = 512
-CHUNKS = (384, 384, 128, 128)
+GROUPS = ((0, 512), (512, 256), (768, 256))
+CH = 256
+N_PIVOT = 3
 
 
 def tile_picked_wmedian_relu_l_kernel(tc, x_words, x_scales, w1, pos1, pos2, pos3, out):
@@ -32,29 +34,48 @@ def tile_picked_wmedian_relu_l_kernel(tc, x_words, x_scales, w1, pos1, pos2, pos
         nc.vector.memset(planes[:].bitcast(I32), 0)
         warm = keep.tile([P, 8], F32, name="warm")
         warm_out = keep.tile([P, 8], F32, name="warm_out")
-        nc.gpsimd.memset(warm[:], 0.0)
+        nc.vector.memset(warm[:], 0.0)
+        ident = keep.tile([P, P], F32, name="ident")
+        nc.vector.memset(ident[:], 0.0)
+        make_identity(nc, ident[:], nomemset=True)
 
-        w_raw = [keep.tile([P, PACK, M], F32, name="w_raw%d" % z) for z in range(PASSES)]
-        x_sb = [[keep.tile([P, HALF], I32, name="x%d%d" % (z, h), align_bytes=64) for h in range(2)] for z in range(PASSES)]
         w_rows = w1.rearrange("(z p j) m -> z p j m", z=PASSES, j=PACK)
         x_i32 = x_words.rearrange("z p c r -> z p (c r)").bitcast(I32)
         s_i32 = x_scales.bitcast(I32)
 
-        for q in range(4):
-            nc.scalar.dma_start(out=planes[32 * q : 32 * q + 8, :].bitcast(I32), in_=s_i32[:, 4 * q : 4 * q + 4, :])
+        def load_scales(queue, q):
+            queue.dma_start(out=planes[32 * q : 32 * q + 8, :].bitcast(I32), in_=s_i32[:, 4 * q : 4 * q + 4, :])
+
+        x_sb = {}
+
+        def load_x(z, c0, n):
+            xt = keep.tile([P, n], I32, name="x%d_%d" % (z, c0), align_bytes=64)
+            nc.sync.dma_start(out=xt[:], in_=x_i32[z][:, c0 : c0 + n])
+            for g0, gn in GROUPS:
+                if c0 <= g0 and g0 + gn <= c0 + n:
+                    x_sb[(z, g0)] = xt[:, g0 - c0 : g0 - c0 + gn]
+
+        load_scales(nc.scalar, 0)
+        load_scales(nc.scalar, 1)
         nc.scalar.activation(warm_out[:], warm[:], ACT.Relu)
 
-        nc.sync.dma_start(out=w_raw[0][:], in_=w_rows[0])
-        nc.sync.dma_start(out=x_sb[0][0][:], in_=x_i32[0][:, 0:HALF])
-        nc.sync.dma_start(out=w_raw[1][:], in_=w_rows[1])
-        nc.sync.dma_start(out=x_sb[1][0][:], in_=x_i32[1][:, 0:HALF])
-        nc.sync.dma_start(out=x_sb[0][1][:], in_=x_i32[0][:, HALF:T])
-        nc.sync.dma_start(out=x_sb[1][1][:], in_=x_i32[1][:, HALF:T])
+        w_raw = []
+        for z in range(PASSES):
+            raw = keep.tile([P, PACK, M], F32, name="w_raw%d" % z)
+            nc.sync.dma_start(out=raw[:], in_=w_rows[z])
+            w_raw.append(raw)
+        load_scales(nc.sync, 2)
+        load_scales(nc.sync, 3)
+        load_x(0, 0, 512)
+        load_x(1, 0, 512)
+        load_x(0, 512, 512)
         lists = []
-        for i, pos in enumerate((pos1, pos2, pos3)):
+        for i, pos in enumerate((pos2, pos3, pos1)):
             offs = keep.tile([P, T // 16], U16, name="offs%d" % i)
             nc.sync.dma_start(offs[:], pos)
             lists.append(offs)
+        load_x(1, 512, 256)
+        load_x(1, 768, 256)
 
         w_codes = []
         w_scales = []
@@ -71,40 +92,100 @@ def tile_picked_wmedian_relu_l_kernel(tc, x_words, x_scales, w1, pos1, pos2, pos
             w_scales.append(scales)
 
         y = keep.tile([P, T], F32, name="y")
-        Q = 256
-        groups = [(0, 0, HALF), (1, 0, Q), (1, Q, Q)]
-        for g, (h, c0, n) in enumerate(groups):
-            acc = psum.tile([P, n], F32, name="acc%d" % g)
+        for g, (c0, n) in enumerate(GROUPS):
+            acc = psum.tile([P, n], F32, name="acc%d" % g, tag=("o0", "o1", "vb1")[g])
             for z in range(PASSES):
                 nc.tensor.matmul_mx(
                     out=acc[:],
                     lhsT=w_codes[z][:].bitcast(FP8X4),
                     lhsT_scale=w_scales[z][:],
-                    rhs=x_sb[z][h][:, c0 : c0 + n].bitcast(FP8X4),
-                    rhs_scale=planes[4 * z : P, h * HALF + c0 : h * HALF + c0 + n],
+                    rhs=x_sb[(z, c0)].bitcast(FP8X4),
+                    rhs_scale=planes[4 * z : P, c0 : c0 + n],
                     start=(z == 0),
                     stop=(z == PASSES - 1),
                 )
-            dst = y[:, h * HALF + c0 : h * HALF + c0 + n]
             if g == 2:
-                nc.vector.tensor_scalar(dst, acc[:], 0.0, None, ALU.max)
+                nc.vector.tensor_scalar(y[:, c0 : c0 + n], acc[:], 0.0, None, ALU.max)
             else:
-                nc.scalar.activation(dst, acc[:], ACT.Relu)
+                nc.scalar.activation(y[:, c0 : c0 + n], acc[:], ACT.Relu)
 
-        v0 = 0
-        for i, n in enumerate(CHUNKS):
-            got = []
-            for l in range(3):
-                gt = keep.tile([P, n], F32, name="g%d_%d" % (i, l))
-                nc.vector.tensor_copy(gt[:], y[:].indirect(lists[l][:, v0 // 16 : (v0 + n) // 16]))
-                got.append(gt)
-            lo = keep.tile([P, n], F32, name="lo%d" % i)
-            hi = keep.tile([P, n], F32, name="hi%d" % i)
-            up = keep.tile([P, n], F32, name="up%d" % i)
-            res = keep.tile([P, n], F32, name="res%d" % i)
-            nc.vector.tensor_tensor(hi[:], got[0][:], got[1][:], ALU.max)
-            nc.vector.tensor_tensor(lo[:], got[0][:], got[1][:], ALU.min)
-            nc.vector.tensor_tensor(up[:], hi[:], got[2][:], ALU.min)
-            nc.vector.tensor_tensor(res[:], lo[:], up[:], ALU.max)
-            nc.sync.dma_start(out=out[:, v0 : v0 + n], in_=res[:])
-            v0 = v0 + n
+        def fresh(name):
+            return keep.tile([P, CH], F32, name=name)[:]
+
+        def gather(dst, l, i):
+            nc.vector.tensor_copy(dst, y[:].indirect(lists[l][:, i * CH // 16 : (i + 1) * CH // 16]))
+            return dst
+
+        def turn(dst, src, start, stop):
+            nc.tensor.matmul(dst, src, ident[:], start=start, stop=stop, is_transpose=True)
+
+        blocks = [slice(j, j + P) for j in range(0, CH, P)]
+        a, b, c, nb, u, v_sb, b_sb, t1 = {}, {}, {}, {}, {}, {}, {}, {}
+
+        def turned_sum(name, tag, first, second):
+            bank = psum.tile([P, CH], F32, name=name, tag=tag)
+            for blk in blocks:
+                turn(bank[:, blk], first[:, blk], True, False)
+                turn(bank[:, blk], second[:, blk], False, True)
+            return bank
+
+        def negate(i, dst):
+            nb[i] = dst
+            nc.scalar.activation(nb[i], b[i], ACT.Copy, scale=-1.0)
+
+        def after_c(i):
+            vp = turned_sum("vp%d" % i, "vb%d" % (i % 2), nb[i], c[i])
+            v_sb[i] = fresh("v_sb%d" % i)
+            nc.scalar.copy(v_sb[i], vp[:])
+            bp = psum.tile([P, CH], F32, name="bp%d" % i, tag="bp%d" % (i % 2))
+            for blk in blocks:
+                turn(bp[:, blk], b[i][:, blk], True, True)
+            b_sb[i] = fresh("b_sb%d" % i)
+            nc.scalar.copy(b_sb[i], bp[:])
+
+        def after_a(i):
+            u[i] = turned_sum("u%d" % i, "u%d" % (i % 2), nb[i], a[i])
+
+        def lower(i):
+            t1[i] = fresh("t1_%d" % i)
+            nc.vector.scalar_tensor_tensor(t1[i], u[i][:], 0.0, v_sb[i], ALU.min, ALU.max)
+
+        def upper(i):
+            t2 = fresh("t2_%d" % i)
+            nc.vector.scalar_tensor_tensor(t2, u[i][:], 0.0, t1[i], ALU.max, ALU.min)
+            o = turned_sum("o%d" % i, "o%d" % (i % 2), b_sb[i], t2)
+            res = fresh("res%d" % i)
+            nc.scalar.copy(res, o[:])
+            nc.sync.dma_start(out=out[:, i * CH : (i + 1) * CH], in_=res)
+
+        for i in range(2):
+            b[i] = gather(fresh("b%d" % i), 0, i)
+            negate(i, fresh("nb%d" % i))
+            c[i] = gather(fresh("c%d" % i), 1, i)
+            after_c(i)
+            a[i] = gather(fresh("a%d" % i), 2, i)
+            after_a(i)
+        b[2] = gather(fresh("b2"), 0, 2)
+        negate(2, c[1])
+        lower(0)
+        c[2] = gather(a[0], 1, 2)
+        upper(0)
+        after_c(2)
+        a[2] = gather(v_sb[0], 2, 2)
+        after_a(2)
+        b[3] = gather(t1[0], 0, 3)
+        lower(1)
+        c[3] = gather(a[1], 1, 3)
+        upper(1)
+        lower(2)
+        hi = a[2]
+        nc.vector.tensor_tensor(hi, b[3], c[3], ALU.max)
+        upper(2)
+        a[3] = gather(v_sb[2], 2, 3)
+        lo = t1[2]
+        up = fresh("up")
+        res = fresh("dres")
+        nc.vector.tensor_tensor(lo, b[3], c[3], ALU.min)
+        nc.vector.tensor_tensor(up, hi, a[3], ALU.min)
+        nc.vector.tensor_tensor(res, lo, up, ALU.max)
+        nc.sync.dma_start(out=out[:, 3 * CH : 4 * CH], in_=res)

@@ -20,8 +20,7 @@ P = 128
 PACK = 4
 PASSES = 2
 GROUPS = ((0, 512), (512, 256), (768, 256))
-CH = 256
-N_PIVOT = 3
+WIDTHS = (256, 256, 256, 256)
 
 
 def tile_picked_wmedian_relu_l_kernel(tc, x_words, x_scales, w1, pos1, pos2, pos3, out):
@@ -69,13 +68,13 @@ def tile_picked_wmedian_relu_l_kernel(tc, x_words, x_scales, w1, pos1, pos2, pos
         load_x(0, 0, 512)
         load_x(1, 0, 512)
         load_x(0, 512, 512)
+        load_x(1, 512, 256)
+        load_x(1, 768, 256)
         lists = []
         for i, pos in enumerate((pos2, pos3, pos1)):
             offs = keep.tile([P, T // 16], U16, name="offs%d" % i)
             nc.sync.dma_start(offs[:], pos)
             lists.append(offs)
-        load_x(1, 512, 256)
-        load_x(1, 768, 256)
 
         w_codes = []
         w_scales = []
@@ -93,7 +92,7 @@ def tile_picked_wmedian_relu_l_kernel(tc, x_words, x_scales, w1, pos1, pos2, pos
 
         y = keep.tile([P, T], F32, name="y")
         for g, (c0, n) in enumerate(GROUPS):
-            acc = psum.tile([P, n], F32, name="acc%d" % g, tag=("o0", "o1", "vb1")[g])
+            acc = psum.tile([P, n], F32, name="acc%d" % g, tag=("o0", "o1", "u1")[g])
             for z in range(PASSES):
                 nc.tensor.matmul_mx(
                     out=acc[:],
@@ -109,22 +108,26 @@ def tile_picked_wmedian_relu_l_kernel(tc, x_words, x_scales, w1, pos1, pos2, pos
             else:
                 nc.scalar.activation(y[:, c0 : c0 + n], acc[:], ACT.Relu)
 
-        def fresh(name):
-            return keep.tile([P, CH], F32, name=name)[:]
+        starts = [sum(WIDTHS[:i]) for i in range(len(WIDTHS))]
+
+        def fresh(name, n):
+            return keep.tile([P, n], F32, name=name)[:]
 
         def gather(dst, l, i):
-            nc.vector.tensor_copy(dst, y[:].indirect(lists[l][:, i * CH // 16 : (i + 1) * CH // 16]))
+            nc.vector.tensor_copy(dst, y[:].indirect(lists[l][:, starts[i] // 16 : (starts[i] + WIDTHS[i]) // 16]))
             return dst
 
         def turn(dst, src, start, stop):
             nc.tensor.matmul(dst, src, ident[:], start=start, stop=stop, is_transpose=True)
 
-        blocks = [slice(j, j + P) for j in range(0, CH, P)]
-        a, b, c, nb, u, v_sb, b_sb, t1 = {}, {}, {}, {}, {}, {}, {}, {}
+        def blocks(i):
+            return [slice(j, j + P) for j in range(0, WIDTHS[i], P)]
 
-        def turned_sum(name, tag, first, second):
-            bank = psum.tile([P, CH], F32, name=name, tag=tag)
-            for blk in blocks:
+        a, b, c, nb, u, v_sb, b_sb, t1, t2 = {}, {}, {}, {}, {}, {}, {}, {}, {}
+
+        def turned_sum(tag, i, first, second):
+            bank = psum.tile([P, WIDTHS[i]], F32, name="%s_%d" % (tag, i), tag="%s%d" % (tag, i % 2))
+            for blk in blocks(i):
                 turn(bank[:, blk], first[:, blk], True, False)
                 turn(bank[:, blk], second[:, blk], False, True)
             return bank
@@ -133,59 +136,70 @@ def tile_picked_wmedian_relu_l_kernel(tc, x_words, x_scales, w1, pos1, pos2, pos
             nb[i] = dst
             nc.scalar.activation(nb[i], b[i], ACT.Copy, scale=-1.0)
 
-        def after_c(i):
-            vp = turned_sum("vp%d" % i, "vb%d" % (i % 2), nb[i], c[i])
-            v_sb[i] = fresh("v_sb%d" % i)
+        def after_c(i, dst):
+            vp = turned_sum("vb", i, nb[i], c[i])
+            v_sb[i] = dst
             nc.scalar.copy(v_sb[i], vp[:])
-            bp = psum.tile([P, CH], F32, name="bp%d" % i, tag="bp%d" % (i % 2))
-            for blk in blocks:
+            bp = psum.tile([P, WIDTHS[i]], F32, name="bp_%d" % i, tag=("bp0", "vb0", "vb1")[i])
+            for blk in blocks(i):
                 turn(bp[:, blk], b[i][:, blk], True, True)
-            b_sb[i] = fresh("b_sb%d" % i)
+            b_sb[i] = fresh("b_sb%d" % i, WIDTHS[i])
             nc.scalar.copy(b_sb[i], bp[:])
 
         def after_a(i):
-            u[i] = turned_sum("u%d" % i, "u%d" % (i % 2), nb[i], a[i])
+            u[i] = turned_sum("u", i, nb[i], a[i])
 
-        def lower(i):
-            t1[i] = fresh("t1_%d" % i)
+        def lower(i, dst):
+            t1[i] = dst
             nc.vector.scalar_tensor_tensor(t1[i], u[i][:], 0.0, v_sb[i], ALU.min, ALU.max)
 
         def upper(i):
-            t2 = fresh("t2_%d" % i)
-            nc.vector.scalar_tensor_tensor(t2, u[i][:], 0.0, t1[i], ALU.max, ALU.min)
-            o = turned_sum("o%d" % i, "o%d" % (i % 2), b_sb[i], t2)
-            res = fresh("res%d" % i)
-            nc.scalar.copy(res, o[:])
-            nc.sync.dma_start(out=out[:, i * CH : (i + 1) * CH], in_=res)
+            t2[i] = fresh("t2_%d" % i, WIDTHS[i])
+            nc.vector.scalar_tensor_tensor(t2[i], u[i][:], 0.0, t1[i], ALU.max, ALU.min)
 
+        def back(i):
+            o = turned_sum("o", i, b_sb[i], t2[i])
+            res = fresh("res%d" % i, WIDTHS[i])
+            nc.scalar.copy(res, o[:])
+            nc.sync.dma_start(out=out[:, starts[i] : starts[i] + WIDTHS[i]], in_=res)
+
+        w0, w1_, w2, w3 = WIDTHS
         for i in range(2):
-            b[i] = gather(fresh("b%d" % i), 0, i)
-            negate(i, fresh("nb%d" % i))
-            c[i] = gather(fresh("c%d" % i), 1, i)
-            after_c(i)
-            a[i] = gather(fresh("a%d" % i), 2, i)
+            b[i] = gather(fresh("b%d" % i, WIDTHS[i]), 0, i)
+            negate(i, fresh("nb%d" % i, WIDTHS[i]))
+            c[i] = gather(fresh("c%d" % i, WIDTHS[i]), 1, i)
+            after_c(i, fresh("v_sb%d" % i, WIDTHS[i]))
+            a[i] = gather(fresh("a%d" % i, WIDTHS[i]), 2, i)
             after_a(i)
-        b[2] = gather(fresh("b2"), 0, 2)
-        negate(2, c[1])
-        lower(0)
-        c[2] = gather(a[0], 1, 2)
+        b[2] = gather(fresh("b2", w2), 0, 2)
+        negate(2, c[0][:, w0 - w2 : w0])
+        lower(0, fresh("t1_0", w0))
+        c[2] = gather(a[0][:, w0 - w2 : w0], 1, 2)
+        a[3] = fresh("a3", w3)
+        after_c(2, a[3][:, 0:w2])
         upper(0)
-        after_c(2)
-        a[2] = gather(v_sb[0], 2, 2)
+        a[2] = gather(v_sb[0][:, 0:w2], 2, 2)
         after_a(2)
-        b[3] = gather(t1[0], 0, 3)
-        lower(1)
+        back(0)
+        b[3] = gather(t1[0][:, 0:w3], 0, 3)
+        lower(1, fresh("t1_1", w1_))
         c[3] = gather(a[1], 1, 3)
         upper(1)
-        lower(2)
-        hi = a[2]
+        back(1)
+        lo = fresh("lo", w3)
+        lower(2, lo[:, 0:w2])
+        hi = v_sb[0][:, 0:w3]
         nc.vector.tensor_tensor(hi, b[3], c[3], ALU.max)
         upper(2)
-        a[3] = gather(v_sb[2], 2, 3)
-        lo = t1[2]
-        up = fresh("up")
-        res = fresh("dres")
+        back(2)
+        gather(a[3], 2, 3)
         nc.vector.tensor_tensor(lo, b[3], c[3], ALU.min)
-        nc.vector.tensor_tensor(up, hi, a[3], ALU.min)
-        nc.vector.tensor_tensor(res, lo, up, ALU.max)
-        nc.sync.dma_start(out=out[:, 3 * CH : 4 * CH], in_=res)
+        halves = blocks(3)
+        ups = [fresh("up%d" % h, P) for h in range(2)]
+        for h, blk in enumerate(halves):
+            nc.vector.tensor_tensor(ups[h], hi[:, blk], a[3][:, blk], ALU.min)
+        for h, blk in enumerate(halves):
+            res = fresh("dres%d" % h, P)
+            nc.vector.tensor_tensor(res, lo[:, blk], ups[h], ALU.max)
+            queue = nc.sync if h == 0 else nc.scalar
+            queue.dma_start(out=out[:, starts[3] + h * P : starts[3] + (h + 1) * P], in_=res)

@@ -127,9 +127,9 @@ def tile_picked_wmedian_relu_l_kernel(tc, x_words, x_scales, w1, pos1, pos2, pos
 
         def turned_sum(tag, i, first, second):
             bank = psum.tile([P, WIDTHS[i]], F32, name="%s_%d" % (tag, i), tag="%s%d" % (tag, i % 2))
-            for blk in blocks(i):
-                turn(bank[:, blk], first[:, blk], True, False)
-                turn(bank[:, blk], second[:, blk], False, True)
+            steps = [(src, blk) for src in (first, second) for blk in blocks(i)]
+            for j, (src, blk) in enumerate(steps):
+                turn(bank[:, blk], src[:, blk], j == 0, j == len(steps) - 1)
             return bank
 
         def negate(i, dst):

from contextlib import ExitStack

import concourse.mybir as mybir
from concourse.masks import make_identity

K, T, M = 1024, 1024, 128
FLOPS = 2 * K * T * M

F32 = mybir.dt.float32
BF16 = mybir.dt.bfloat16
I32 = mybir.dt.int32
U32 = mybir.dt.uint32
U16 = mybir.dt.uint16
U8 = mybir.dt.uint8
FP8X4 = mybir.dt.float8_e4m3fn_x4
ALU = mybir.AluOpType
ACT = mybir.ActivationFunctionType

P = 128
PACK = 4
PASSES = 2
GROUPS = ((0, 512), (512, 256), (768, 256))
WIDTHS = (256, 256, 256, 256)


def tile_picked_wmedian_relu_l_kernel(tc, x_words, x_scales, w1, pos1, pos2, pos3, out):
    nc = tc.nc
    with ExitStack() as ctx:
        keep = ctx.enter_context(tc.tile_pool(name="keep", bufs=1))
        psum = ctx.enter_context(tc.psum_pool(name="psum", bufs=1))

        planes = keep.tile([P, T], U8, name="planes", align_bytes=64)
        nc.vector.memset(planes[:].bitcast(I32), 0)
        warm = keep.tile([P, 8], F32, name="warm")
        warm_out = keep.tile([P, 8], F32, name="warm_out")
        nc.vector.memset(warm[:], 0.0)
        ident = keep.tile([P, P], F32, name="ident")
        nc.vector.memset(ident[:], 0.0)
        make_identity(nc, ident[:], nomemset=True)

        w_rows = w1.rearrange("(z p j) m -> z p j m", z=PASSES, j=PACK)
        x_i32 = x_words.rearrange("z p c r -> z p (c r)").bitcast(I32)
        s_i32 = x_scales.bitcast(I32)

        def load_scales(queue, q):
            queue.dma_start(out=planes[32 * q : 32 * q + 8, :].bitcast(I32), in_=s_i32[:, 4 * q : 4 * q + 4, :])

        x_sb = {}

        def load_x(z, c0, n):
            xt = keep.tile([P, n], I32, name="x%d_%d" % (z, c0), align_bytes=64)
            nc.sync.dma_start(out=xt[:], in_=x_i32[z][:, c0 : c0 + n])
            for g0, gn in GROUPS:
                if c0 <= g0 and g0 + gn <= c0 + n:
                    x_sb[(z, g0)] = xt[:, g0 - c0 : g0 - c0 + gn]

        load_scales(nc.scalar, 0)
        load_scales(nc.scalar, 1)
        nc.scalar.activation(warm_out[:], warm[:], ACT.Relu)

        w_raw = []
        for z in range(PASSES):
            raw = keep.tile([P, PACK, M], F32, name="w_raw%d" % z)
            nc.sync.dma_start(out=raw[:], in_=w_rows[z])
            w_raw.append(raw)
        load_scales(nc.sync, 2)
        load_scales(nc.sync, 3)
        load_x(0, 0, 512)
        load_x(1, 0, 512)
        load_x(0, 512, 512)
        load_x(1, 512, 256)
        load_x(1, 768, 256)
        lists = []
        for i, pos in enumerate((pos2, pos3, pos1)):
            offs = keep.tile([P, T // 16], U16, name="offs%d" % i)
            nc.sync.dma_start(offs[:], pos)
            lists.append(offs)

        w_codes = []
        w_scales = []
        for z in range(PASSES):
            grouped = keep.tile([P, M, PACK], BF16, name="grouped%d" % z, align_bytes=64)
            nc.vector.tensor_copy(
                out=grouped[:].rearrange("p (c i) j -> p c j i", i=4),
                in_=w_raw[z][:].rearrange("p j (c i) -> p c j i", i=4),
            )
            codes = keep.tile([P, M], U32, name="w_codes%d" % z, align_bytes=64)
            scales = keep.tile([P, M], U8, name="w_scales%d" % z, align_bytes=64)
            nc.vector.quantize_mx(out=codes[:].bitcast(FP8X4), scales=scales[:], in_=grouped[:].rearrange("p m j -> p (m j)"))
            w_codes.append(codes)
            w_scales.append(scales)

        y = keep.tile([P, T], F32, name="y")
        for g, (c0, n) in enumerate(GROUPS):
            acc = psum.tile([P, n], F32, name="acc%d" % g, tag=("o0", "o1", "u1")[g])
            for z in range(PASSES):
                nc.tensor.matmul_mx(
                    out=acc[:],
                    lhsT=w_codes[z][:].bitcast(FP8X4),
                    lhsT_scale=w_scales[z][:],
                    rhs=x_sb[(z, c0)].bitcast(FP8X4),
                    rhs_scale=planes[4 * z : P, c0 : c0 + n],
                    start=(z == 0),
                    stop=(z == PASSES - 1),
                )
            if g == 2:
                nc.vector.tensor_scalar(y[:, c0 : c0 + n], acc[:], 0.0, None, ALU.max)
            else:
                nc.scalar.activation(y[:, c0 : c0 + n], acc[:], ACT.Relu)

        starts = [sum(WIDTHS[:i]) for i in range(len(WIDTHS))]

        def fresh(name, n):
            return keep.tile([P, n], F32, name=name)[:]

        def gather(dst, l, i):
            nc.vector.tensor_copy(dst, y[:].indirect(lists[l][:, starts[i] // 16 : (starts[i] + WIDTHS[i]) // 16]))
            return dst

        def turn(dst, src, start, stop):
            nc.tensor.matmul(dst, src, ident[:], start=start, stop=stop, is_transpose=True)

        def blocks(i):
            return [slice(j, j + P) for j in range(0, WIDTHS[i], P)]

        a, b, c, nb, u, v_sb, b_sb, t1, t2 = {}, {}, {}, {}, {}, {}, {}, {}, {}

        def turned_sum(tag, i, first, second):
            bank = psum.tile([P, WIDTHS[i]], F32, name="%s_%d" % (tag, i), tag="%s%d" % (tag, i % 2))
            steps = [(src, blk) for src in (first, second) for blk in blocks(i)]
            for j, (src, blk) in enumerate(steps):
                turn(bank[:, blk], src[:, blk], j == 0, j == len(steps) - 1)
            return bank

        def negate(i, dst):
            nb[i] = dst
            nc.scalar.activation(nb[i], b[i], ACT.Copy, scale=-1.0)

        def after_c(i, dst):
            vp = turned_sum("vb", i, nb[i], c[i])
            v_sb[i] = dst
            nc.scalar.copy(v_sb[i], vp[:])
            bp = psum.tile([P, WIDTHS[i]], F32, name="bp_%d" % i, tag=("bp0", "vb0", "vb1")[i])
            for blk in blocks(i):
                turn(bp[:, blk], b[i][:, blk], True, True)
            b_sb[i] = fresh("b_sb%d" % i, WIDTHS[i])
            nc.scalar.copy(b_sb[i], bp[:])

        def after_a(i):
            u[i] = turned_sum("u", i, nb[i], a[i])

        def lower(i, dst):
            t1[i] = dst
            nc.vector.scalar_tensor_tensor(t1[i], u[i][:], 0.0, v_sb[i], ALU.min, ALU.max)

        def upper(i):
            t2[i] = fresh("t2_%d" % i, WIDTHS[i])
            nc.vector.scalar_tensor_tensor(t2[i], u[i][:], 0.0, t1[i], ALU.max, ALU.min)

        def back(i):
            o = turned_sum("o", i, b_sb[i], t2[i])
            res = fresh("res%d" % i, WIDTHS[i])
            nc.scalar.copy(res, o[:])
            nc.sync.dma_start(out=out[:, starts[i] : starts[i] + WIDTHS[i]], in_=res)

        w0, w1_, w2, w3 = WIDTHS
        for i in range(2):
            b[i] = gather(fresh("b%d" % i, WIDTHS[i]), 0, i)
            negate(i, fresh("nb%d" % i, WIDTHS[i]))
            c[i] = gather(fresh("c%d" % i, WIDTHS[i]), 1, i)
            after_c(i, fresh("v_sb%d" % i, WIDTHS[i]))
            a[i] = gather(fresh("a%d" % i, WIDTHS[i]), 2, i)
            after_a(i)
        b[2] = gather(fresh("b2", w2), 0, 2)
        negate(2, c[0][:, w0 - w2 : w0])
        lower(0, fresh("t1_0", w0))
        c[2] = gather(a[0][:, w0 - w2 : w0], 1, 2)
        a[3] = fresh("a3", w3)
        after_c(2, a[3][:, 0:w2])
        upper(0)
        a[2] = gather(v_sb[0][:, 0:w2], 2, 2)
        after_a(2)
        back(0)
        b[3] = gather(t1[0][:, 0:w3], 0, 3)
        lower(1, fresh("t1_1", w1_))
        c[3] = gather(a[1], 1, 3)
        upper(1)
        back(1)
        lo = fresh("lo", w3)
        lower(2, lo[:, 0:w2])
        hi = v_sb[0][:, 0:w3]
        nc.vector.tensor_tensor(hi, b[3], c[3], ALU.max)
        upper(2)
        back(2)
        gather(a[3], 2, 3)
        nc.vector.tensor_tensor(lo, b[3], c[3], ALU.min)
        halves = blocks(3)
        ups = [fresh("up%d" % h, P) for h in range(2)]
        for h, blk in enumerate(halves):
            nc.vector.tensor_tensor(ups[h], hi[:, blk], a[3][:, blk], ALU.min)
        for h, blk in enumerate(halves):
            res = fresh("dres%d" % h, P)
            nc.vector.tensor_tensor(res, lo[:, blk], ups[h], ALU.max)
            queue = nc.sync if h == 0 else nc.scalar
            queue.dma_start(out=out[:, starts[3] + h * P : starts[3] + (h + 1) * P], in_=res)
